import numpy as np, ml_dtypes
CORES = [3,7,11,15,131,135,139,143]
N = 8
import mx_ref
BF = ml_dtypes.bfloat16
def pick(q, e):
    c = np.concatenate([q[0].reshape(128, -1, 4), np.zeros((128, 1, 4), np.uint8)], axis=1); s = np.concatenate([q[1], np.ones((16, 1), np.uint8)], axis=1)
    return (np.ascontiguousarray(c[:, e].reshape(128, -1)), np.ascontiguousarray(s[:, e]))
def join(*qs):
    return (np.concatenate([q[0] for q in qs], axis=1), np.concatenate([q[1] for q in qs], axis=1))
def put(q, e, v):
    c, s = q[0].reshape(128, -1, 4).copy(), q[1].copy(); c[:, e] = v[0].reshape(128, -1, 4); s[:, e] = v[1]
    return (c.reshape(128, -1), s)
def pk(c, s):
    return (np.ascontiguousarray(c), mx_ref.live(s))
def emit(q):
    return q[0], q[1]
def cols(t, e):
    v = np.concatenate([t.reshape(128, -1, 4), np.zeros((128, 1, 4), BF)], axis=1)
    return np.ascontiguousarray(v[:, e]).reshape(128, -1)
def tile(rs):
    return np.stack(rs, axis=2).reshape(128, -1).astype(BF)
def decode(q):
    o = []
    for b in range(4):
        e = np.zeros((128, 128, 4), np.float32); e[np.arange(128), np.arange(128), b] = 1
        o.append(mx_ref.matmul(mx_ref.quantize(e.reshape(128, 512).astype(BF)), q))
    return np.stack(o, axis=2).reshape(128, -1)
def f(rng, *shape):
    return mx_ref.flush((rng.standard_normal(shape, dtype=np.float32) * np.exp2(rng.integers(-2, 3, shape[:-1] + (1,)))).astype(BF))
def wide(rng, *shape, cols=0):
    v = rng.standard_normal(shape, dtype=np.float32) * np.exp2(rng.integers(-12, 13, shape)).astype(np.float32)
    if cols: v *= np.repeat(np.exp2(rng.integers(-cols, cols + 1, shape[:-2] + (1, shape[-1] // 4))) * (rng.random(shape[:-2] + (1, shape[-1] // 4)) > 0.0625), 4, axis=-1).astype(np.float32)
    return mx_ref.flush(v.astype(BF))
P, K, R = 128, 16, 2
def times(t, v):
    return mx_ref.flush((t.astype(np.float32) * np.asarray(v, np.float32) + np.float32(0)).astype(BF))
def columns(v):
    return mx_ref.flush(np.ascontiguousarray(v.reshape(-1, 128, 4).transpose(1, 0, 2)).reshape(128, -1).astype(np.float32).astype(BF))
def plain(rng):
    return {"x": times(f(rng, N, 128, 4 * P), 64), "u": f(rng, N, 128, 4), "w": f(rng, N, 128, 512)}
def setup_inputs(rng):
    return plain(rng)
def setup_inputs_shadow(rng):
    d, H, xs, us = plain(rng), K // 2, [], []
    for r in range(N):
        way = rng.choice([-1.0, 1.0], 512)
        q = np.where(np.arange(512) < 480, way, 0.0)
        q[480], q[481] = 2.0 ** -14, 2.0 ** -16
        line, at = rng.permutation(480), rng.permutation(P)
        v = rng.standard_normal((P, 512)) * 2.0 ** -4
        v[at[:3 * H + 4 + K]] = 0
        for e, level in ((np.sort(at[:H]), 1.0), (np.sort(at[H:2 * H + 4]), 0.875), (at[2 * H + 4:3 * H + 4], 0.75)):
            for g, j in enumerate(e):
                k = line[16 * (g % H):16 * (g % H) + 16]
                v[j, k] = level * way[k]
                if level > 0.75: v[j, 480], v[j, 481] = 0.25 * (g // 4), 0.25 * (g % 4)
        for j in at[3 * H + 4:3 * H + 4 + K]:
            k = line[16 * H + rng.permutation(480 - 16 * H)[:16]]
            v[j, k] = 0.625 * way[k]
        v = v * rng.choice([-1.0, 1.0], (P, 1))
        xs.append(columns(v * np.exp2(rng.integers(4, 9))))
        us.append(columns(q[None] * np.exp2(rng.integers(-3, 4))))
    return {**d, "x": np.stack(xs), "u": np.stack(us)}
def setup_inputs_ties(rng):
    d = plain(rng)
    d["x"] = np.stack([times(cols(d["x"][r], rng.permutation(np.arange(P) % 6)), np.repeat(rng.choice([-1.0, 1.0], P), 4)) for r in range(N)])
    return d
def setup_inputs_few(rng):
    d = plain(rng)
    n = 8 * rng.integers(K // 8, R * K // 8, N) + rng.integers(4, 8, N)
    p = rng.permutation(N)
    n[p[0]], n[p[1]] = 3, P
    d["x"] = np.stack([times(d["x"][r], 2.0 ** -14 * np.repeat(rng.permutation(P) < n[r], 4)) for r in range(N)])
    return d
def setup_inputs_huge(rng):
    d, xs, us = plain(rng), [], []
    lean = 0.5 + 0.5 * np.sqrt(3.6 / (K - 1))
    for r in range(N):
        way = rng.choice([-1.0, 1.0], 512)
        us.append(columns((way * (1.75 + 0.25 * rng.random(512)) * 2.0 ** 29)[None]))
        v = way * np.where(rng.random((P, 512)) < lean, 1.0, -1.0) * rng.choice([-1.0, 1.0], (P, 1))
        xs.append(columns(v * (1 + rng.random((P, 512))) * 2.0 ** 27))
    return {**d, "x": np.stack(xs), "u": np.stack(us)}
def setup_inputs_spread(rng):
    return {**plain(rng), "x": wide(rng, N, 128, 4 * P, cols=6)}
def check_inputs(d):
    b = []
    for k in ("x", "u", "w"):
        v = np.abs(d[k].astype(np.float32))
        if not (np.isfinite(v).all() and ((v == 0) | (v >= 2.0 ** -30) & (v <= 2.0 ** 30)).all()): b.append("a value of " + k)
    return b
UP = 2.0 ** np.arange(-64, 74)
DOWN = 2.0 ** -np.arange(-64.0, 74)
def play(x, u):
    ask = [mx_ref.quantize(np.concatenate([u[r], np.zeros((128, 508), BF)], axis=1)) for r in range(N)]
    X = mx_ref.quantize(np.concatenate([x[r] for r in range(N)], axis=1))
    free, rounds = np.ones((N, P), bool), []
    for t in range(R):
        at, took = np.full(128, -1), np.zeros((N, K), int)
        for r in range(N):
            s = np.abs(mx_ref.matmul(ask[r], pick(X, P * r + np.arange(P)))[0])
            o = np.argsort(np.where(free[r], 0.0 - s, np.inf), kind="stable")[:K]
            free[r, o] = False
            at[r * K:r * K + K] = P * r + o
            took[r] = o
        m = pick(X, at)
        rounds.append((took, m))
        d = np.diagonal(mx_ref.matmul(m, m))
        h = np.where(d > 0, DOWN[np.maximum(np.searchsorted(UP, d, side="right") - 1, 0)], 0.0).astype(np.float32)
        c = np.zeros((128, N * P, 4), np.float32)
        c[:, :, 0] = mx_ref.matmul(m, X) * h[:, None]
        c = mx_ref.quantize(c.reshape(128, -1).astype(BF))
        dx, parts = decode(X).reshape(128, N * P, 4), []
        dm = np.concatenate([dx, np.zeros((128, 1, 4), np.float32)], axis=1)[:, at]
        for b in range(4):
            mt = np.zeros((128, 128, 4), np.float32)
            mt[:, :, 0] = dm[:, :, b].T
            z = mx_ref.matmul(mx_ref.quantize(mt.reshape(128, 512).astype(BF)), c)
            parts.append(dx[:, :, b] - np.float32(0.25) * z)
        X = mx_ref.quantize(tile(parts))
    return X, rounds
def reference(x, u, w):
    y, pl = np.zeros((N, 128, R * N * K), np.float32), np.zeros((N, 1, R * K), np.float32)
    oc, osc = np.zeros((N, 128, 4 * P), np.uint8), np.zeros((N, 16, P), np.uint8)
    own = [mx_ref.quantize(np.ascontiguousarray(w[r])) for r in range(N)]
    X, rounds = play(x, u)
    for t in range(R):
        took, m = rounds[t]
        for r in range(N):
            pl[r, 0, t * K:t * K + K] = took[r]
            y[r, :, t * N * K:(t + 1) * N * K] = mx_ref.matmul(own[r], m)[:, :N * K]
    for r in range(N):
        oc[r], osc[r] = emit(pick(X, P * r + np.arange(P)))
    return {"y": y, "pl": pl, "oc": oc, "osc": osc}

@@ -1,0 +1,260 @@
+import numpy as np
+from concourse.bass import DstId, RemoteDMATransfer
+from concourse.mybir import dt, AluOpType, AxisListType, ActivationFunctionType
+
+P, K, R = 128, 16, 2
+CODE, PLANE, BF, F32 = "float8_e4m3fn_x4", "uint8", "bfloat16", "float32"
+BIG = 2.0 ** 99
+
+
+def _sb(n, d):
+    return ("sbuf", [128, n], d)
+
+
+SCRATCH = {
+    "xb": _sb(512, BF), "ub": _sb(4, BF), "wb": _sb(512, BF), "ut": _sb(512, BF),
+    "sgn": _sb(128, BF), "ew": _sb(520, BF), "mt": _sb(2048, BF), "ct": _sb(512, BF), "rt": _sb(512, BF),
+    "uq": _sb(128, CODE), "us": _sb(128, PLANE), "wq": _sb(128, CODE), "ws": _sb(128, PLANE),
+    "eq": _sb(512, CODE), "es": _sb(512, PLANE), "mtq": _sb(512, CODE), "mts": _sb(512, PLANE),
+    "cq": _sb(128, CODE), "cs": _sb(128, PLANE),
+    "xq0": _sb(128, CODE), "xs0": _sb(128, PLANE), "xq1": _sb(128, CODE), "xs1": _sb(128, PLANE),
+    "xq2": _sb(128, CODE), "xs2": _sb(128, PLANE),
+    "mq0": _sb(128, CODE), "ms0": _sb(128, PLANE), "mq1": _sb(128, CODE), "ms1": _sb(128, PLANE),
+    "dif": _sb(128, BF), "phi": _sb(128, F32), "one": _sb(160, BF), "cm": _sb(160, BF), "sm": _sb(160, BF), "vv": _sb(32, BF),
+    "lt": _sb(128, F32), "big": _sb(16, F32), "bm": _sb(128, F32), "af": _sb(128, F32),
+    "thr": _sb(4, F32), "prd": _sb(4, F32), "pen": _sb(4, F32), "of": _sb(4, F32), "om": _sb(4, F32),
+    "off0": _sb(2, "uint16"), "off1": _sb(2, "uint16"), "pl0": _sb(4, F32), "pl1": _sb(4, F32),
+    "dr": _sb(132, F32), "qc": _sb(4, F32), "sc": _sb(4, F32), "hc": _sb(4, F32),
+    "y0": _sb(128, F32), "y1": _sb(128, F32),
+    "pr0": ("psum", [128, 512], F32), "pr1": ("psum", [128, 512], F32), "pr2": ("psum", [128, 512], F32), "pr3": ("psum", [128, 512], F32),
+    "ps": ("psum", [128, 512], F32), "pd": ("psum", [128, 512], F32), "pa": ("psum", [128, 512], F32), "pb": ("psum", [128, 512], F32),
+}
+SEMAPHORES = ["sv", "ss", "st", "sg", "lx", "lu", "lw", "so", "sp", "loc", "earr", "arr0", "arr1"]
+
+
+def rank_program(g, core, T, topo):
+    rank = T.rank_of(core)
+    if rank is None:
+        return
+    A, F = AluOpType, ActivationFunctionType
+    sem = T.sem
+    queues = {"v": g.vector, "s": g.scalar, "t": g.tensor, "g": g, "y": g.sync}
+    count, seen = {}, {}
+
+    def need(q, *toks):
+        for s, n in toks:
+            if seen.get((q, s), 0) < n:
+                queues[q].wait_ge(sem[s], n)
+                seen[(q, s)] = n
+
+    def done(ins, s, n=1):
+        count[s] = count.get(s, 0) + n
+        ins.then_inc(sem[s], n)
+        return (s, count[s])
+
+    def V(ins):
+        return done(ins, "sv")
+
+    def S(ins):
+        return done(ins, "ss")
+
+    def M(out, l, ls, r, rs, start=True, stop=True):
+        return done(g.tensor.matmul_mx(out, l, ls, r, rs, start, stop), "st")
+
+    peers = [d for d in T.cores if d != core]
+    mate = [d for d in topo.cores_of(core) if d in peers][0]
+    far = sorted([d for d in peers if d != mate], key=lambda d: (-((T.rank_of(d) ^ rank) >> 1), T.rank_of(d) ^ rank))
+    fmask = topo.mask(core, mate)
+    for d in far:
+        fmask &= topo.mask(core, d)
+    near = [e for e in topo.engines(core, mate) if not fmask >> e & 1]
+    nmask = (1 << near[0]) | (1 << near[len(near) // 2])
+    bits = lambda m: bin(m).count("1")
+    half = 0 if core < mate else 1
+
+    def dst(d):
+        rid, pid = topo.addr(d, core)
+        return DstId(rid=rid, pnc=pid)
+
+    def send(src, s, *groups):
+        g.remote_dma_fused([RemoteDMATransfer(dst_ids=[dst(d) for d in to], dma_engine_mask=m, remote_sem=sem[s],
+                                              srcs=[src], dsts=[src for d in to]) for to, m in groups], local_sem=sem.loc)
+        count["loc"] = count.get("loc", 0) + sum(bits(m) for to, m in groups)
+
+    def codes(b, a, e):
+        return T[b][:, a:e].bitcast(dt.uint8)
+
+    enum, anum = bits(fmask) + bits(nmask), 2 * (6 * bits(fmask) + bits(nmask))
+
+    lu = done(g.scalar.dma_start(T.ub[:], T.u[:]), "lu", 16)
+    lx = done(g.sync.dma_start(T.xb[:], T.x[:]), "lx", 16)
+    need("y", lx)
+    lw = done(g.sync.dma_start(T.wb[:], T.w[:]), "lw", 16)
+
+    G = lambda ins: done(ins, "sg")
+    small = {"allow_small_or_imprecise_dtypes": True}
+    kj = G(g.iota(T.dif[:], [[1, 128]], 0, -1, **small))
+    kc = G(g.iota(T.cm[:, 128:129], [[0, 1]], 0, 1, **small))
+
+    ve = V(g.vector.memset(T.ew[:], 0.0))
+    need("v", ve, kj)
+    v = V(g.vector.tensor_scalar(T.ew[:, 3:515:4], T.dif[:], 0.0, -4.0, A.is_equal, A.mult))
+    need("v", v)
+
+    def make_e(b):
+        return V(g.vector.quantize_mx(T.eq[:, 128 * b:128 * b + 128], T.es[:, 128 * b:128 * b + 128], T.ew[:, 3 - b:515 - b]))
+
+    te = make_e(half)
+    need("g", te)
+    send(codes("eq", 128 * half, 128 * half + 128), "earr", ([mate], fmask))
+    send(T.es[:, 128 * half:128 * half + 128], "earr", ([mate], nmask))
+
+    def zeros(i):
+        return S(g.scalar.activation(T.mt[:, 512 * i:512 * i + 512], T.ct[:], F.Copy))
+
+    vs = V(g.vector.memset(T.sgn[:], 1.0))
+    vz = V(g.vector.memset(T.ct[:], 0.0))
+    need("s", vz)
+    zeros(0)
+    v1 = V(g.vector.memset(T.one[:], 1.0))
+    need("v", vs)
+    vs = V(g.vector.memset(T.sgn[:, 1:2], -1.0))
+    need("v", v1)
+    V(g.vector.memset(T.one[:, 127:128], 256.0))
+    need("v", lu, vs)
+    for i in range(4):
+        v = V(g.vector.tensor_scalar(T.ut[:, i:512:4], T.sgn[:], T.ub[:, i:i + 1], None, A.mult))
+    need("v", v)
+    tu = V(g.vector.quantize_mx(T.uq[:], T.us[:], T.ut[:]))
+    need("v", lx)
+    tx = V(g.vector.quantize_mx(T.xq0[:], T.xs0[:], T.xb[:]))
+    V(g.vector.tensor_scalar(T.lt[:], T.dif[:], 0.0, -BIG, A.is_lt, A.mult))
+    need("v", kc)
+    v = V(g.vector.memset(T.cm[:, 129:160], -256.0))
+    need("v", v)
+    vc = V(g.vector.memset(T.cm[:, 144:145], 3840.0))
+
+    own = (K * rank, K * rank + K)
+    sread, ty, sy = [], None, None
+    for t in range(R):
+        xq, xs, mq, ms = "xq%d" % t, "xs%d" % t, "mq%d" % t, "ms%d" % t
+        off, pl = T["off%d" % t], T["pl%d" % t]
+        need("t", tu, tx, *sread)
+        ts = M(T.ps[:, 0:128], T.uq[:], T.us[:], T[xq][:], T[xs][:])
+        tc = M(T.pa[:, 0:128], T[xq][:], T[xs][:], T.uq[:], T.us[:])
+        need("s", ts)
+        sabs = S(g.scalar.activation(T.af[:], T.ps[:, 0:128], F.Abs, bias=2.0 ** -120))
+        need("v", tc)
+        V(g.vector.tensor_scalar(T.thr[:, 0:1], T.pa[:, 0:1], T.pa[:, 1:2], 2.0 ** -120, A.max, A.max))
+        v = V(g.vector.tensor_scalar(T.prd[:, 0:1], T.pa[:, 0:1], T.pa[:, 1:2], 1.0 - 2.0 ** -24, A.max, A.mult))
+        need("v", v)
+        v = V(g.vector.tensor_scalar(T.bm[:], T.lt[:], T.thr[:, 0:1], T.prd[:, 0:1], A.add, A.max))
+        need("v", v, sabs)
+        v = V(g.vector.tensor_tensor(T.cm[:, 0:128], T.af[:], T.bm[:], A.is_gt))
+        need("v", v)
+        v = V(g.vector.tensor_tensor_scan(T.sm[:], T.cm[:], T.one[:], 0.0, A.add, A.mult))
+        need("v", v)
+        v = V(g.vector.transpose(T.vv[:], T.sm[:, 128:160]))
+        need("v", v)
+        v = V(g.vector.tensor_reduce(T.of[:, 0:1], T.vv[:], AxisListType.X, A.min, apply_absolute_value=True))
+        need("v", v)
+        vm = V(g.vector.tensor_scalar(T.om[0:64, 0:1], T.of[0:64, 0:1], T.of[64:128, 0:1], None, A.min))
+        need("v", vm)
+        for a in range(4):
+            voff = V(g.vector.tensor_scalar(off[32 * a:32 * a + 32, 0:1], T.om[0:32, 0:1], T.om[32:64, 0:1], None, A.min))
+        need("v", voff)
+        tp = V(g.vector.tensor_copy(T[mq][:, own[0]:own[1]].bitcast(dt.uint32), T[xq][:, 0:128].bitcast(dt.uint32).indirect(off[:, 0:1])))
+        need("s", voff)
+        tq = S(g.scalar.activation(T[ms][:, own[0]:own[1]], T[xs][:, 0:128].indirect(off[:, 0:1]), F.Copy))
+        need("g", tp)
+        send(codes(mq, own[0], own[1]), "arr%d" % t, (far, fmask), ([mate], nmask))
+        need("g", tq)
+        send(T[ms][:, own[0]:own[1]], "arr%d" % t, (far, fmask), ([mate], nmask))
+        def copy_y(r):
+            need("s", ty)
+            s = S(g.scalar.activation(T["y%d" % r][:], T.pd[:, 0:128], F.Copy))
+            need("y", s)
+            done(g.sync.dma_start(T.y[:, P * r:P * r + P], T["y%d" % r][:]), "so", 16)
+            return s
+
+        if t == 0:
+            zeros(1)
+            zm = zeros(2)
+            make_e(2)
+            te = make_e(3)
+            V(g.vector.memset(T.mt[:, 1536:2048], 0.0))
+            V(g.vector.tensor_scalar(T.phi[:], T.dif[:], 0.0, 2.0 ** 23 + 1, A.is_equal, A.mult))
+            V(g.vector.memset(T.dr[:, 128:132], 2.0 ** -45))
+            vb = V(g.vector.memset(T.big[:], BIG))
+        else:
+            sy = copy_y(0)
+        vp = V(g.vector.tensor_scalar(pl[0:32, 0:1], T.om[0:32, 0:1], T.om[32:64, 0:1], None, A.min))
+        need("y", vp)
+        done(g.sync.dma_start(T.pl[0:1, K * t:K * t + K], pl[0:16, 0:1]), "so", 16)
+        if t == 0:
+            v = V(g.vector.tensor_scalar(T.pen[:, 0:1], T.sm[:, 128:129], 4096.0, 16384.0, A.is_lt, A.mult))
+            need("v", lw)
+            tw = V(g.vector.quantize_mx(T.wq[:], T.ws[:], T.wb[:]))
+            need("v", v)
+            V(g.vector.tensor_scalar(T.cm[:, 128:129], T.cm[:, 128:129], T.pen[:, 0:1], None, A.add))
+            V(g.vector.tensor_copy(T.lt[:, 0:128].indirect(off[:, 0:1]), T.big[:]))
+        need("t", te, ("earr", enum))
+        for b in range(4):
+            M(T["pr%d" % b][:, 0:128], T.eq[:, 128 * b:128 * b + 128], T.es[:, 128 * b:128 * b + 128], T[xq][:], T[xs][:], True, False)
+        need("t", tp, tq, ("arr%d" % t, anum), sabs)
+        if sy:
+            need("t", sy)
+        td = M(T.pd[:, 0:128], T[mq][:], T[ms][:], T[mq][:], T[ms][:])
+        ta = M(T.pa[:, 0:256], T[mq][:], T[ms][:], T.eq[:, 0:256], T.es[:, 0:256])
+        tg = M(T.ps[:, 0:128], T[mq][:], T[ms][:], T[xq][:], T[xs][:])
+        tb = M(T.pb[:, 0:256], T[mq][:], T[ms][:], T.eq[:, 256:512], T.es[:, 256:512])
+        need("s", zm, ta, ("sv", count["sv"]))
+        sa = S(g.scalar.activation(T.mt[:, 0:1024:4], T.pa[:, 0:256], F.Copy, scale=-0.25))
+        need("s", tb)
+        sb = S(g.scalar.activation(T.mt[:, 1024:2048:4], T.pb[:, 0:256], F.Copy, scale=-0.25))
+        need("v", td, zm, ("sv", count["sv"]))
+        vd = V(g.vector.tensor_tensor(T.dr[:, 0:128], T.pd[:, 0:128], T.phi[:], A.mult))
+        need("v", vd)
+        v = V(g.vector.tensor_reduce(T.qc[:, 0:1], T.dr[:, 0:129], AxisListType.X, A.max))
+        need("v", v)
+        v = V(g.vector.tensor_scalar(T.sc[:, 0:1], T.qc[:, 0:1], -(1.0 - 2.0 ** -24), T.qc[:, 0:1], A.mult, A.add))
+        need("v", v)
+        v = V(g.vector.reciprocal(T.hc[:, 0:1], T.sc[:, 0:1]))
+        need("v", v, tg)
+        v = V(g.vector.tensor_scalar(T.ct[:, 0:512:4], T.ps[:, 0:128], T.hc[:, 0:1], None, A.mult))
+        need("v", v)
+        qc = V(g.vector.quantize_mx(T.cq[:], T.cs[:], T.ct[:]))
+        need("v", sa)
+        q0 = V(g.vector.quantize_mx(T.mtq[:, 0:256], T.mts[:, 0:256], T.mt[:, 0:1024]))
+        need("v", sb)
+        q2 = V(g.vector.quantize_mx(T.mtq[:, 256:384], T.mts[:, 256:384], T.mt[:, 1024:1536]))
+        q3 = V(g.vector.quantize_mx(T.mtq[:, 384:512], T.mts[:, 384:512], T.mt[:, 1536:2048]))
+        need("t", tw, vd)
+        ty = M(T.pd[:, 0:128], T.wq[:], T.ws[:], T[mq][:], T[ms][:])
+        if t:
+            copy_y(t)
+        tz = []
+        for b in range(4):
+            need("t", qc, (q0, q0, q2, q3)[b])
+            tz.append(M(T["pr%d" % b][:, 0:128], T.mtq[:, 128 * b:128 * b + 128], T.mts[:, 128 * b:128 * b + 128], T.cq[:], T.cs[:], False, True))
+        for b in range(4):
+            q = "ssvv"[b]
+            need(q, tz[b])
+            src, out = T["pr%d" % b][:, 0:128], T.rt[:, b:512:4]
+            if q == "s":
+                s = S(g.scalar.activation(out, src, F.Copy, scale=-0.25))
+            else:
+                v = V(g.vector.tensor_scalar(out, src, -0.25, None, A.mult))
+        need("v", s, v)
+        tx = V(g.vector.quantize_mx(T["xq%d" % (t + 1)][:], T["xs%d" % (t + 1)][:], T.rt[:]))
+        sread = [sa, sb]
+
+    need("y", tx)
+    need("s", tx)
+    xs = T["xs%d" % R]
+    done(g.sync.dma_start(T.oc[:], codes("xq%d" % R, 0, 128)), "so", 16)
+    for k in range(4):
+        q, s = (g.scalar, "sp") if k % 2 == 0 else (g.sync, "so")
+        done(q.dma_start(T.osc[4 * k:4 * k + 4, :], xs[32 * k:32 * k + 4, :]), s, 16)
+    need("g", *[(s, n) for s, n in count.items()])
+    need("g", ("earr", enum), ("arr0", anum), ("arr1", anum))

@@ -5,6 +5,7 @@ from concourse.mybir import dt, AluOpType, AxisListType, ActivationFunctionType
 P, K, R = 128, 16, 2
 CODE, PLANE, BF, F32 = "float8_e4m3fn_x4", "uint8", "bfloat16", "float32"
 BIG = 2.0 ** 99
+NH = 136
 
 
 def _sb(n, d):
@@ -20,11 +21,11 @@ SCRATCH = {
     "xq0": _sb(128, CODE), "xs0": _sb(128, PLANE), "xq1": _sb(128, CODE), "xs1": _sb(128, PLANE),
     "xq2": _sb(128, CODE), "xs2": _sb(128, PLANE),
     "mq0": _sb(128, CODE), "ms0": _sb(128, PLANE), "mq1": _sb(128, CODE), "ms1": _sb(128, PLANE),
-    "dif": _sb(128, BF), "phi": _sb(128, F32), "one": _sb(160, BF), "cm": _sb(160, BF), "sm": _sb(160, BF), "vv": _sb(32, BF),
-    "lt": _sb(128, F32), "big": _sb(16, F32), "bm": _sb(128, F32), "af": _sb(128, F32),
-    "thr": _sb(4, F32), "prd": _sb(4, F32), "pen": _sb(4, F32), "of": _sb(4, F32), "om": _sb(4, F32),
+    "dif": _sb(128, BF), "phi": _sb(128, F32), "one": _sb(160, BF), "cm": _sb(160, BF), "sm": _sb(160, BF), "vv": _sb(64, BF),
+    "lt": _sb(128, F32), "fac": _sb(128, F32), "big": _sb(16, F32), "bm": _sb(128, F32), "af": _sb(128, F32),
+    "thr": _sb(4, F32), "prd": _sb(4, F32), "pen": _sb(4, F32), "om": _sb(4, F32),
     "off0": _sb(2, "uint16"), "off1": _sb(2, "uint16"), "pl0": _sb(4, F32), "pl1": _sb(4, F32),
-    "dr": _sb(132, F32), "qc": _sb(4, F32), "sc": _sb(4, F32), "hc": _sb(4, F32),
+    "dr": _sb(128, BF), "dm": _sb(128, BF), "up": _sb(NH, BF), "two": _sb(NH, BF), "zr": _sb(NH, BF), "hf": _sb(NH, BF), "hs": _sb(NH, BF),
     "y0": _sb(128, F32), "y1": _sb(128, F32),
     "pr0": ("psum", [128, 512], F32), "pr1": ("psum", [128, 512], F32), "pr2": ("psum", [128, 512], F32), "pr3": ("psum", [128, 512], F32),
     "ps": ("psum", [128, 512], F32), "pd": ("psum", [128, 512], F32), "pa": ("psum", [128, 512], F32), "pb": ("psum", [128, 512], F32),
@@ -99,6 +100,7 @@ def rank_program(g, core, T, topo):
     ve = V(g.vector.memset(T.ew[:], 0.0))
     need("v", ve, kj)
     v = V(g.vector.tensor_scalar(T.ew[:, 3:515:4], T.dif[:], 0.0, -4.0, A.is_equal, A.mult))
+    vs = V(g.vector.memset(T.sgn[:], 1.0))
     need("v", v)
 
     def make_e(b):
@@ -112,27 +114,22 @@ def rank_program(g, core, T, topo):
     def zeros(i):
         return S(g.scalar.activation(T.mt[:, 512 * i:512 * i + 512], T.ct[:], F.Copy))
 
-    vs = V(g.vector.memset(T.sgn[:], 1.0))
+    need("v", vs)
+    vs = V(g.vector.memset(T.sgn[:, 1:2], -1.0))
     vz = V(g.vector.memset(T.ct[:], 0.0))
     need("s", vz)
     zeros(0)
-    v1 = V(g.vector.memset(T.one[:], 1.0))
-    need("v", vs)
-    vs = V(g.vector.memset(T.sgn[:, 1:2], -1.0))
-    need("v", v1)
-    V(g.vector.memset(T.one[:, 127:128], 256.0))
     need("v", lu, vs)
     for i in range(4):
         v = V(g.vector.tensor_scalar(T.ut[:, i:512:4], T.sgn[:], T.ub[:, i:i + 1], None, A.mult))
+    v1 = V(g.vector.memset(T.one[:], 1.0))
     need("v", v)
     tu = V(g.vector.quantize_mx(T.uq[:], T.us[:], T.ut[:]))
     need("v", lx)
     tx = V(g.vector.quantize_mx(T.xq0[:], T.xs0[:], T.xb[:]))
-    V(g.vector.tensor_scalar(T.lt[:], T.dif[:], 0.0, -BIG, A.is_lt, A.mult))
-    need("v", kc)
-    v = V(g.vector.memset(T.cm[:, 129:160], -256.0))
-    need("v", v)
-    vc = V(g.vector.memset(T.cm[:, 144:145], 3840.0))
+    V(g.vector.tensor_scalar(T.fac[:], T.dif[:], 0.0, 1.0 - 2.0 ** -24, A.is_ge, A.max))
+    need("v", v1)
+    V(g.vector.memset(T.one[:, 127:128], 256.0))
 
     own = (K * rank, K * rank + K)
     sread, ty, sy = [], None, None
@@ -145,20 +142,27 @@ def rank_program(g, core, T, topo):
         need("s", ts)
         sabs = S(g.scalar.activation(T.af[:], T.ps[:, 0:128], F.Abs, bias=2.0 ** -120))
         need("v", tc)
-        V(g.vector.tensor_scalar(T.thr[:, 0:1], T.pa[:, 0:1], T.pa[:, 1:2], 2.0 ** -120, A.max, A.max))
-        v = V(g.vector.tensor_scalar(T.prd[:, 0:1], T.pa[:, 0:1], T.pa[:, 1:2], 1.0 - 2.0 ** -24, A.max, A.mult))
-        need("v", v)
-        v = V(g.vector.tensor_scalar(T.bm[:], T.lt[:], T.thr[:, 0:1], T.prd[:, 0:1], A.add, A.max))
+        v = V(g.vector.tensor_scalar(T.thr[:, 0:1], T.pa[:, 0:1], T.pa[:, 1:2], 2.0 ** -120, A.max, A.max))
+        if t == 0:
+            need("v", kc)
+            vc = V(g.vector.memset(T.cm[:, 129:160], -256.0))
+            need("v", v)
+            v = V(g.vector.tensor_scalar(T.bm[:], T.fac[:], T.thr[:, 0:1], None, A.mult))
+            need("v", vc)
+            V(g.vector.memset(T.cm[:, 144:145], 3840.0))
+        else:
+            v = V(g.vector.tensor_scalar(T.prd[:, 0:1], T.pa[:, 0:1], T.pa[:, 1:2], 1.0 - 2.0 ** -24, A.max, A.mult))
+            need("v", v)
+            v = V(g.vector.tensor_scalar(T.bm[:], T.lt[:], T.thr[:, 0:1], T.prd[:, 0:1], A.add, A.max))
         need("v", v, sabs)
         v = V(g.vector.tensor_tensor(T.cm[:, 0:128], T.af[:], T.bm[:], A.is_gt))
         need("v", v)
         v = V(g.vector.tensor_tensor_scan(T.sm[:], T.cm[:], T.one[:], 0.0, A.add, A.mult))
         need("v", v)
-        v = V(g.vector.transpose(T.vv[:], T.sm[:, 128:160]))
+        V(g.vector.transpose(T.vv[0:64, 0:32], T.sm[0:64, 128:160]))
+        v = V(g.vector.transpose(T.vv[0:64, 32:64], T.sm[64:128, 128:160]))
         need("v", v)
-        v = V(g.vector.tensor_reduce(T.of[:, 0:1], T.vv[:], AxisListType.X, A.min, apply_absolute_value=True))
-        need("v", v)
-        vm = V(g.vector.tensor_scalar(T.om[0:64, 0:1], T.of[0:64, 0:1], T.of[64:128, 0:1], None, A.min))
+        vm = V(g.vector.tensor_reduce(T.om[0:64, 0:1], T.vv[0:64, 0:64], AxisListType.X, A.min, apply_absolute_value=True))
         need("v", vm)
         for a in range(4):
             voff = V(g.vector.tensor_scalar(off[32 * a:32 * a + 32, 0:1], T.om[0:32, 0:1], T.om[32:64, 0:1], None, A.min))
@@ -180,11 +184,15 @@ def rank_program(g, core, T, topo):
         if t == 0:
             zeros(1)
             zm = zeros(2)
+            V(g.vector.memset(T.two[:], 2.0))
+            v = V(g.vector.memset(T.zr[:], 0.0))
             make_e(2)
             te = make_e(3)
+            V(g.vector.tensor_scalar(T.lt[:], T.dif[:], 0.0, -BIG, A.is_lt, A.mult))
             V(g.vector.memset(T.mt[:, 1536:2048], 0.0))
-            V(g.vector.tensor_scalar(T.phi[:], T.dif[:], 0.0, 2.0 ** 23 + 1, A.is_equal, A.mult))
-            V(g.vector.memset(T.dr[:, 128:132], 2.0 ** -45))
+            V(g.vector.tensor_scalar(T.phi[:], T.dif[:], 0.0, 1.0 + 3.0 / 256, A.is_equal, A.mult))
+            need("v", v)
+            V(g.vector.tensor_tensor_scan(T.up[:], T.two[:], T.zr[:], 2.0 ** -64 * (1.0 + 1.0 / 64), A.mult, A.max))
             vb = V(g.vector.memset(T.big[:], BIG))
         else:
             sy = copy_y(0)
@@ -205,37 +213,41 @@ def rank_program(g, core, T, topo):
         if sy:
             need("t", sy)
         td = M(T.pd[:, 0:128], T[mq][:], T[ms][:], T[mq][:], T[ms][:])
-        ta = M(T.pa[:, 0:256], T[mq][:], T[ms][:], T.eq[:, 0:256], T.es[:, 0:256])
+        ta = M(T.pa[:, 0:128], T[mq][:], T[ms][:], T.eq[:, 0:128], T.es[:, 0:128])
+        tb = M(T.pb[:, 0:384], T[mq][:], T[ms][:], T.eq[:, 128:512], T.es[:, 128:512])
         tg = M(T.ps[:, 0:128], T[mq][:], T[ms][:], T[xq][:], T[xs][:])
-        tb = M(T.pb[:, 0:256], T[mq][:], T[ms][:], T.eq[:, 256:512], T.es[:, 256:512])
         need("s", zm, ta, ("sv", count["sv"]))
-        sa = S(g.scalar.activation(T.mt[:, 0:1024:4], T.pa[:, 0:256], F.Copy, scale=-0.25))
+        sa = S(g.scalar.activation(T.mt[:, 0:512:4], T.pa[:, 0:128], F.Copy, scale=-0.25))
         need("s", tb)
-        sb = S(g.scalar.activation(T.mt[:, 1024:2048:4], T.pb[:, 0:256], F.Copy, scale=-0.25))
+        s1 = S(g.scalar.activation(T.mt[:, 512:1024:4], T.pb[:, 0:128], F.Copy, scale=-0.25))
+        sb = S(g.scalar.activation(T.mt[:, 1024:2048:4], T.pb[:, 128:384], F.Copy, scale=-0.25))
+
+        def turned(b):
+            need("v", (sa, s1, sb, sb)[b])
+            return V(g.vector.quantize_mx(T.mtq[:, 128 * b:128 * b + 128], T.mts[:, 128 * b:128 * b + 128], T.mt[:, 512 * b:512 * b + 512]))
+
         need("v", td, zm, ("sv", count["sv"]))
-        vd = V(g.vector.tensor_tensor(T.dr[:, 0:128], T.pd[:, 0:128], T.phi[:], A.mult))
+        vd = V(g.vector.tensor_tensor(T.dr[:], T.pd[:, 0:128], T.phi[:], A.mult))
         need("v", vd)
-        v = V(g.vector.tensor_reduce(T.qc[:, 0:1], T.dr[:, 0:129], AxisListType.X, A.max))
+        v = V(g.vector.tensor_tensor_scan(T.dm[:], T.dr[:], T.zr[:, 0:128], 0.0, A.max, A.max))
         need("v", v)
-        v = V(g.vector.tensor_scalar(T.sc[:, 0:1], T.qc[:, 0:1], -(1.0 - 2.0 ** -24), T.qc[:, 0:1], A.mult, A.add))
+        v = V(g.vector.tensor_scalar(T.hf[:], T.up[:], T.dm[:, 127:128], 0.5, A.is_gt, A.max))
         need("v", v)
-        v = V(g.vector.reciprocal(T.hc[:, 0:1], T.sc[:, 0:1]))
+        v = V(g.vector.tensor_tensor_scan(T.hs[:], T.hf[:], T.zr[:], 2.0 ** 64, A.mult, A.max))
+        qm = [turned(0)]
         need("v", v, tg)
-        v = V(g.vector.tensor_scalar(T.ct[:, 0:512:4], T.ps[:, 0:128], T.hc[:, 0:1], None, A.mult))
+        v = V(g.vector.tensor_scalar(T.ct[:, 0:512:4], T.ps[:, 0:128], T.hs[:, NH - 1:NH], None, A.mult))
+        qm.append(turned(1))
         need("v", v)
         qc = V(g.vector.quantize_mx(T.cq[:], T.cs[:], T.ct[:]))
-        need("v", sa)
-        q0 = V(g.vector.quantize_mx(T.mtq[:, 0:256], T.mts[:, 0:256], T.mt[:, 0:1024]))
-        need("v", sb)
-        q2 = V(g.vector.quantize_mx(T.mtq[:, 256:384], T.mts[:, 256:384], T.mt[:, 1024:1536]))
-        q3 = V(g.vector.quantize_mx(T.mtq[:, 384:512], T.mts[:, 384:512], T.mt[:, 1536:2048]))
+        qm += [turned(2), turned(3)]
         need("t", tw, vd)
         ty = M(T.pd[:, 0:128], T.wq[:], T.ws[:], T[mq][:], T[ms][:])
         if t:
             copy_y(t)
         tz = []
         for b in range(4):
-            need("t", qc, (q0, q0, q2, q3)[b])
+            need("t", qc, qm[b])
             tz.append(M(T["pr%d" % b][:, 0:128], T.mtq[:, 128 * b:128 * b + 128], T.mts[:, 128 * b:128 * b + 128], T.cq[:], T.cs[:], False, True))
         for b in range(4):
             q = "ssvv"[b]

@@ -4,7 +4,8 @@ from concourse.mybir import dt, AluOpType, AxisListType, ActivationFunctionType
 
 P, K, R = 128, 16, 2
 CODE, PLANE, BF, F32 = "float8_e4m3fn_x4", "uint8", "bfloat16", "float32"
-BIG = 2.0 ** 99
+TINY = 2.0 ** -120
+BIG = 2.0 ** 80
 NH = 136
 
 
@@ -15,17 +16,18 @@ def _sb(n, d):
 SCRATCH = {
     "xb": _sb(512, BF), "ub": _sb(4, BF), "wb": _sb(512, BF), "ut": _sb(512, BF),
     "sgn": _sb(128, BF), "ew": _sb(520, BF), "mt": _sb(2048, BF), "ct": _sb(512, BF), "rt": _sb(512, BF),
+    "bt": _sb(512, BF), "kw": _sb(512, BF), "kt": _sb(512, BF),
     "uq": _sb(128, CODE), "us": _sb(128, PLANE), "wq": _sb(128, CODE), "ws": _sb(128, PLANE),
     "eq": _sb(512, CODE), "es": _sb(512, PLANE), "mtq": _sb(512, CODE), "mts": _sb(512, PLANE),
     "cq": _sb(128, CODE), "cs": _sb(128, PLANE),
-    "xq0": _sb(128, CODE), "xs0": _sb(128, PLANE), "xq1": _sb(128, CODE), "xs1": _sb(128, PLANE),
+    "kwq": _sb(128, CODE), "kws": _sb(128, PLANE), "ktq": _sb(128, CODE), "kts": _sb(128, PLANE),
+    "xq0": _sb(384, CODE), "xs0": _sb(384, PLANE), "xq1": _sb(128, CODE), "xs1": _sb(128, PLANE),
     "xq2": _sb(128, CODE), "xs2": _sb(128, PLANE),
     "mq0": _sb(128, CODE), "ms0": _sb(128, PLANE), "mq1": _sb(128, CODE), "ms1": _sb(128, PLANE),
-    "dif": _sb(128, BF), "phi": _sb(128, F32), "one": _sb(160, BF), "cm": _sb(160, BF), "sm": _sb(160, BF), "vv": _sb(64, BF),
-    "lt": _sb(128, F32), "fac": _sb(128, F32), "big": _sb(16, F32), "bm": _sb(128, F32), "af": _sb(128, F32),
-    "thr": _sb(4, F32), "prd": _sb(4, F32), "pen": _sb(4, F32), "om": _sb(4, F32),
+    "dif": _sb(128, BF), "phi": _sb(128, F32), "fac": _sb(128, F32), "nil": _sb(16, F32), "af": _sb(128, F32),
+    "thr": _sb(4, F32), "free": _sb(4, F32),
     "off0": _sb(2, "uint16"), "off1": _sb(2, "uint16"), "pl0": _sb(4, F32), "pl1": _sb(4, F32),
-    "dr": _sb(128, BF), "dm": _sb(128, BF), "up": _sb(NH, BF), "two": _sb(NH, BF), "zr": _sb(NH, BF), "hf": _sb(NH, BF), "hs": _sb(NH, BF),
+    "dm": _sb(128, BF), "up": _sb(NH, BF), "two": _sb(NH, BF), "zr": _sb(NH, BF), "hf": _sb(NH, BF), "hs": _sb(NH, BF),
     "y0": _sb(128, F32), "y1": _sb(128, F32),
     "pr0": ("psum", [128, 512], F32), "pr1": ("psum", [128, 512], F32), "pr2": ("psum", [128, 512], F32), "pr3": ("psum", [128, 512], F32),
     "ps": ("psum", [128, 512], F32), "pd": ("psum", [128, 512], F32), "pa": ("psum", [128, 512], F32), "pb": ("psum", [128, 512], F32),
@@ -95,13 +97,14 @@ def rank_program(g, core, T, topo):
     G = lambda ins: done(ins, "sg")
     small = {"allow_small_or_imprecise_dtypes": True}
     kj = G(g.iota(T.dif[:], [[1, 128]], 0, -1, **small))
-    kc = G(g.iota(T.cm[:, 128:129], [[0, 1]], 0, 1, **small))
+    kk = G(g.iota(T.kw[:, 3:512:4], [[0, 8], [-2, 16]], 0, 0, **small))
 
     ve = V(g.vector.memset(T.ew[:], 0.0))
+    vb = V(g.vector.memset(T.bt[:], -0.25 * TINY))
     need("v", ve, kj)
-    v = V(g.vector.tensor_scalar(T.ew[:, 3:515:4], T.dif[:], 0.0, -4.0, A.is_equal, A.mult))
+    ve = V(g.vector.tensor_scalar(T.ew[:, 3:515:4], T.dif[:], 0.0, -4.0, A.is_equal, A.mult))
     vs = V(g.vector.memset(T.sgn[:], 1.0))
-    need("v", v)
+    need("v", ve)
 
     def make_e(b):
         return V(g.vector.quantize_mx(T.eq[:, 128 * b:128 * b + 128], T.es[:, 128 * b:128 * b + 128], T.ew[:, 3 - b:515 - b]))
@@ -110,66 +113,75 @@ def rank_program(g, core, T, topo):
     need("g", te)
     send(codes("eq", 128 * half, 128 * half + 128), "earr", ([mate], fmask))
     send(T.es[:, 128 * half:128 * half + 128], "earr", ([mate], nmask))
+    eh = (T.eq[:, 128 * half:128 * half + 128], T.es[:, 128 * half:128 * half + 128])
 
-    def zeros(i):
-        return S(g.scalar.activation(T.mt[:, 512 * i:512 * i + 512], T.ct[:], F.Copy))
+    def zeros(out):
+        return S(g.scalar.activation(out, T.ew[:, 0:512], F.Copy, scale=0.0))
 
+    need("s", ve)
+    zeros(T.ct[:])
+    for i in range(3):
+        zeros(T.mt[:, 512 * i:512 * i + 512])
+    qb = V(g.vector.quantize_mx(T.xq0[:, 128:256], T.xs0[:, 128:256], T.bt[:]))
     need("v", vs)
     vs = V(g.vector.memset(T.sgn[:, 1:2], -1.0))
-    vz = V(g.vector.memset(T.ct[:], 0.0))
-    need("s", vz)
-    zeros(0)
     need("v", lu, vs)
     for i in range(4):
         v = V(g.vector.tensor_scalar(T.ut[:, i:512:4], T.sgn[:], T.ub[:, i:i + 1], None, A.mult))
-    v1 = V(g.vector.memset(T.one[:], 1.0))
+    V(g.vector.memset(T.kw[:, 0:512:4], 256.0))
     need("v", v)
     tu = V(g.vector.quantize_mx(T.uq[:], T.us[:], T.ut[:]))
     need("v", lx)
-    tx = V(g.vector.quantize_mx(T.xq0[:], T.xs0[:], T.xb[:]))
-    V(g.vector.tensor_scalar(T.fac[:], T.dif[:], 0.0, 1.0 - 2.0 ** -24, A.is_ge, A.max))
-    need("v", v1)
-    V(g.vector.memset(T.one[:, 127:128], 256.0))
+    tx = V(g.vector.quantize_mx(T.xq0[:, 256:384], T.xs0[:, 256:384], T.xb[:]))
+    vf = V(g.vector.tensor_scalar(T.fac[:], T.dif[:], 0.0, 1.0 - 2.0 ** -24, A.is_le, A.max))
+    V(g.vector.memset(T.kw[:, 1:512:4], 256.0))
+    V(g.vector.memset(T.kw[:, 2:512:4], 1.0))
+    V(g.vector.memset(T.kt[:, 3:512:4], 1.0))
+    vk = V(g.vector.tensor_scalar(T.kt[:, 2:512:4], T.dif[:], 0.0, None, A.is_gt))
+
+    def floor(bank):
+        M(bank[:, 0:130], eh[0], eh[1], T.xq0[:, 128:258], T.xs0[:, 128:258], True, False)
 
     own = (K * rank, K * rank + K)
     sread, ty, sy = [], None, None
     for t in range(R):
-        xq, xs, mq, ms = "xq%d" % t, "xs%d" % t, "mq%d" % t, "ms%d" % t
+        x0 = 0 if t else 256
+        xq, xs = T["xq%d" % t][:, x0:x0 + 128], T["xs%d" % t][:, x0:x0 + 128]
+        mq, ms = "mq%d" % t, "ms%d" % t
         off, pl = T["off%d" % t], T["pl%d" % t]
         need("t", tu, tx, *sread)
-        ts = M(T.ps[:, 0:128], T.uq[:], T.us[:], T[xq][:], T[xs][:])
-        tc = M(T.pa[:, 0:128], T[xq][:], T[xs][:], T.uq[:], T.us[:])
-        need("s", ts)
-        sabs = S(g.scalar.activation(T.af[:], T.ps[:, 0:128], F.Abs, bias=2.0 ** -120))
-        need("v", tc)
-        v = V(g.vector.tensor_scalar(T.thr[:, 0:1], T.pa[:, 0:1], T.pa[:, 1:2], 2.0 ** -120, A.max, A.max))
         if t == 0:
-            need("v", kc)
-            vc = V(g.vector.memset(T.cm[:, 129:160], -256.0))
-            need("v", v)
-            v = V(g.vector.tensor_scalar(T.bm[:], T.fac[:], T.thr[:, 0:1], None, A.mult))
-            need("v", vc)
-            V(g.vector.memset(T.cm[:, 144:145], 3840.0))
+            floor(T.ps)
+        ts = M(T.ps[:, 0:128], T.uq[:], T.us[:], xq, xs, False, True)
+        tc = M(T.pa[:, 0:128], xq, xs, T.uq[:], T.us[:], t == 0, True)
+        need("v", ts, vf)
+        V(g.vector.tensor_tensor(T.af[:], T.ps[:, 0:128], T.fac[:], A.mult))
+        need("v", tc)
+        if t == 0:
+            v = V(g.vector.tensor_scalar(T.thr[:, 0:1], T.pa[:, 0:1], T.pa[:, 1:2], TINY, A.max, A.max))
         else:
-            v = V(g.vector.tensor_scalar(T.prd[:, 0:1], T.pa[:, 0:1], T.pa[:, 1:2], 1.0 - 2.0 ** -24, A.max, A.mult))
-            need("v", v)
-            v = V(g.vector.tensor_scalar(T.bm[:], T.lt[:], T.thr[:, 0:1], T.prd[:, 0:1], A.add, A.max))
-        need("v", v, sabs)
-        v = V(g.vector.tensor_tensor(T.cm[:, 0:128], T.af[:], T.bm[:], A.is_gt))
+            v = V(g.vector.tensor_scalar(T.thr[:, 0:1], T.pa[:, 0:1], T.pa[:, 1:2], T.free[:, 0:1], A.max, A.mult))
         need("v", v)
-        v = V(g.vector.tensor_tensor_scan(T.sm[:], T.cm[:], T.one[:], 0.0, A.add, A.mult))
+        V(g.vector.tensor_scalar(T.kt[:, 0:512:4], T.af[:], T.thr[:, 0:1], 1.0, A.is_lt, A.subtract))
+        v = V(g.vector.tensor_scalar(T.kt[:, 1:512:4], T.af[:], -1.0, T.thr[:, 0:1], A.mult, A.is_lt))
+        if t == 0:
+            need("v", kk)
+            V(g.vector.quantize_mx(T.kwq[:], T.kws[:], T.kw[:]))
         need("v", v)
-        V(g.vector.transpose(T.vv[0:64, 0:32], T.sm[0:64, 128:160]))
-        v = V(g.vector.transpose(T.vv[0:64, 32:64], T.sm[64:128, 128:160]))
-        need("v", v)
-        vm = V(g.vector.tensor_reduce(T.om[0:64, 0:1], T.vv[0:64, 0:64], AxisListType.X, A.min, apply_absolute_value=True))
-        need("v", vm)
-        for a in range(4):
-            voff = V(g.vector.tensor_scalar(off[32 * a:32 * a + 32, 0:1], T.om[0:32, 0:1], T.om[32:64, 0:1], None, A.min))
+        qk = V(g.vector.quantize_mx(T.ktq[:], T.kts[:], T.kt[:]))
+        need("t", qk)
+        tk = M(T.pb[:, 0:128], T.kwq[:], T.kws[:], T.ktq[:], T.kts[:])
+        if t == 0:
+            tr = M(T.pa[:, 0:128], T.ktq[:], T.kts[:], T.kwq[:], T.kws[:])
+            V(g.vector.memset(T.two[:], 2.0))
+            vz = V(g.vector.memset(T.zr[:], 0.0))
+            V(g.vector.memset(T.phi[:], 1.0))
+        need("v", tk)
+        voff = V(g.vector.tensor_reduce(off[:, 0:1], T.pb[:, 0:128], AxisListType.X, A.min, apply_absolute_value=True))
         need("v", voff)
-        tp = V(g.vector.tensor_copy(T[mq][:, own[0]:own[1]].bitcast(dt.uint32), T[xq][:, 0:128].bitcast(dt.uint32).indirect(off[:, 0:1])))
+        tp = V(g.vector.tensor_copy(T[mq][:, own[0]:own[1]].bitcast(dt.uint32), xq.bitcast(dt.uint32).indirect(off[:, 0:1])))
         need("s", voff)
-        tq = S(g.scalar.activation(T[ms][:, own[0]:own[1]], T[xs][:, 0:128].indirect(off[:, 0:1]), F.Copy))
+        tq = S(g.scalar.activation(T[ms][:, own[0]:own[1]], xs.indirect(off[:, 0:1]), F.Copy))
         need("g", tp)
         send(codes(mq, own[0], own[1]), "arr%d" % t, (far, fmask), ([mate], nmask))
         need("g", tq)
@@ -182,40 +194,36 @@ def rank_program(g, core, T, topo):
             return s
 
         if t == 0:
-            zeros(1)
-            zm = zeros(2)
-            V(g.vector.memset(T.two[:], 2.0))
-            v = V(g.vector.memset(T.zr[:], 0.0))
+            zm = zeros(T.mt[:, 1536:2048])
+            v = V(g.vector.tensor_scalar(T.bt[:, half:512:4], T.dif[:], 0.0, BIG, A.not_equal, A.mult))
             make_e(2)
             te = make_e(3)
-            V(g.vector.tensor_scalar(T.lt[:], T.dif[:], 0.0, -BIG, A.is_lt, A.mult))
-            V(g.vector.memset(T.mt[:, 1536:2048], 0.0))
-            V(g.vector.tensor_scalar(T.phi[:], T.dif[:], 0.0, 1.0 + 3.0 / 256, A.is_equal, A.mult))
             need("v", v)
+            qb = V(g.vector.quantize_mx(T.xq0[:, 0:128], T.xs0[:, 0:128], T.bt[:]))
+            V(g.vector.memset(T.phi[:, 127:128], 1.0 + 3.0 / 256))
             V(g.vector.tensor_tensor_scan(T.up[:], T.two[:], T.zr[:], 2.0 ** -64 * (1.0 + 1.0 / 64), A.mult, A.max))
-            vb = V(g.vector.memset(T.big[:], BIG))
+            vn = V(g.vector.memset(T.nil[:], 0.0))
         else:
             sy = copy_y(0)
-        vp = V(g.vector.tensor_scalar(pl[0:32, 0:1], T.om[0:32, 0:1], T.om[32:64, 0:1], None, A.min))
+        vp = V(g.vector.tensor_copy(pl[0:32, 0:1], off[0:32, 0:1]))
         need("y", vp)
         done(g.sync.dma_start(T.pl[0:1, K * t:K * t + K], pl[0:16, 0:1]), "so", 16)
         if t == 0:
-            v = V(g.vector.tensor_scalar(T.pen[:, 0:1], T.sm[:, 128:129], 4096.0, 16384.0, A.is_lt, A.mult))
-            need("v", lw)
+            need("v", tr, lw, vn)
+            vp = V(g.vector.tensor_scalar(T.free[:, 0:1], T.pa[:, 0:1], 4096.0, None, A.is_ge))
             tw = V(g.vector.quantize_mx(T.wq[:], T.ws[:], T.wb[:]))
-            need("v", v)
-            V(g.vector.tensor_scalar(T.cm[:, 128:129], T.cm[:, 128:129], T.pen[:, 0:1], None, A.add))
-            V(g.vector.tensor_copy(T.lt[:, 0:128].indirect(off[:, 0:1]), T.big[:]))
-        need("t", te, ("earr", enum))
+            V(g.vector.tensor_copy(T.fac[:, 0:128].indirect(off[:, 0:1]), T.nil[:]))
+        need("t", te, qb, ("earr", enum))
         for b in range(4):
-            M(T["pr%d" % b][:, 0:128], T.eq[:, 128 * b:128 * b + 128], T.es[:, 128 * b:128 * b + 128], T[xq][:], T[xs][:], True, False)
-        need("t", tp, tq, ("arr%d" % t, anum), sabs)
+            M(T["pr%d" % b][:, 0:128], T.eq[:, 128 * b:128 * b + 128], T.es[:, 128 * b:128 * b + 128], xq, xs, True, False)
         if sy:
             need("t", sy)
-        td = M(T.pd[:, 0:128], T[mq][:], T[ms][:], T[mq][:], T[ms][:])
+        M(T.pd[:, 0:258], eh[0], eh[1], T.xq0[:, 0:258], T.xs0[:, 0:258], True, False)
+        need("t", tp, vp, tq, ("arr%d" % t, anum))
+        td = M(T.pd[:, 0:128], T[mq][:], T[ms][:], T[mq][:], T[ms][:], False, True)
         ta = M(T.pa[:, 0:128], T[mq][:], T[ms][:], T.eq[:, 0:128], T.es[:, 0:128])
         tb = M(T.pb[:, 0:384], T[mq][:], T[ms][:], T.eq[:, 128:512], T.es[:, 128:512])
-        tg = M(T.ps[:, 0:128], T[mq][:], T[ms][:], T[xq][:], T[xs][:])
+        tg = M(T.ps[:, 0:128], T[mq][:], T[ms][:], xq, xs)
         need("s", zm, ta, ("sv", count["sv"]))
         sa = S(g.scalar.activation(T.mt[:, 0:512:4], T.pa[:, 0:128], F.Copy, scale=-0.25))
         need("s", tb)
@@ -227,24 +235,26 @@ def rank_program(g, core, T, topo):
             return V(g.vector.quantize_mx(T.mtq[:, 128 * b:128 * b + 128], T.mts[:, 128 * b:128 * b + 128], T.mt[:, 512 * b:512 * b + 512]))
 
         need("v", td, zm, ("sv", count["sv"]))
-        vd = V(g.vector.tensor_tensor(T.dr[:], T.pd[:, 0:128], T.phi[:], A.mult))
+        vd = V(g.vector.tensor_tensor_scan(T.dm[:], T.pd[:, 0:128], T.phi[:], 0.0, A.max, A.mult))
         need("v", vd)
-        v = V(g.vector.tensor_tensor_scan(T.dm[:], T.dr[:], T.zr[:, 0:128], 0.0, A.max, A.max))
-        need("v", v)
         v = V(g.vector.tensor_scalar(T.hf[:], T.up[:], T.dm[:, 127:128], 0.5, A.is_gt, A.max))
         need("v", v)
         v = V(g.vector.tensor_tensor_scan(T.hs[:], T.hf[:], T.zr[:], 2.0 ** 64, A.mult, A.max))
         qm = [turned(0)]
         need("v", v, tg)
-        v = V(g.vector.tensor_scalar(T.ct[:, 0:512:4], T.ps[:, 0:128], T.hs[:, NH - 1:NH], None, A.mult))
+        vc = V(g.vector.tensor_scalar(T.ct[:, 0:512:4], T.ps[:, 0:128], T.hs[:, NH - 1:NH], None, A.mult))
         qm.append(turned(1))
-        need("v", v)
+        need("v", vc)
         qc = V(g.vector.quantize_mx(T.cq[:], T.cs[:], T.ct[:]))
         qm += [turned(2), turned(3)]
         need("t", tw, vd)
         ty = M(T.pd[:, 0:128], T.wq[:], T.ws[:], T[mq][:], T[ms][:])
         if t:
             copy_y(t)
+        else:
+            need("t", vc, sa)
+            floor(T.ps)
+            floor(T.pa)
         tz = []
         for b in range(4):
             need("t", qc, qm[b])

@@ -13,26 +13,18 @@ def _sb(n, d):
     return ("sbuf", [128, n], d)
 
 
-SCRATCH = {
-    "xb": _sb(512, BF), "ub": _sb(4, BF), "wb": _sb(512, BF), "ut": _sb(512, BF),
-    "sgn": _sb(128, BF), "ew": _sb(520, BF), "mt": _sb(2048, BF), "ct": _sb(512, BF), "rt": _sb(512, BF),
-    "bt": _sb(512, BF), "kw": _sb(512, BF), "kt": _sb(512, BF),
-    "uq": _sb(128, CODE), "us": _sb(128, PLANE), "wq": _sb(128, CODE), "ws": _sb(128, PLANE),
-    "eq": _sb(512, CODE), "es": _sb(512, PLANE), "mtq": _sb(512, CODE), "mts": _sb(512, PLANE),
-    "cq": _sb(128, CODE), "cs": _sb(128, PLANE),
-    "kwq": _sb(128, CODE), "kws": _sb(128, PLANE), "ktq": _sb(128, CODE), "kts": _sb(128, PLANE),
-    "xq0": _sb(384, CODE), "xs0": _sb(384, PLANE), "xq1": _sb(128, CODE), "xs1": _sb(128, PLANE),
-    "xq2": _sb(128, CODE), "xs2": _sb(128, PLANE),
-    "mq0": _sb(128, CODE), "ms0": _sb(128, PLANE), "mq1": _sb(128, CODE), "ms1": _sb(128, PLANE),
-    "dif": _sb(128, BF), "phi": _sb(128, F32), "fac": _sb(128, F32), "nil": _sb(16, F32), "af": _sb(128, F32),
-    "thr": _sb(4, F32), "free": _sb(4, F32),
-    "off0": _sb(2, "uint16"), "off1": _sb(2, "uint16"), "pl0": _sb(4, F32), "pl1": _sb(4, F32),
-    "dm": _sb(128, BF), "up": _sb(NH, BF), "two": _sb(NH, BF), "zr": _sb(NH, BF), "hf": _sb(NH, BF), "hs": _sb(NH, BF),
-    "y0": _sb(128, F32), "y1": _sb(128, F32),
-    "pr0": ("psum", [128, 512], F32), "pr1": ("psum", [128, 512], F32), "pr2": ("psum", [128, 512], F32), "pr3": ("psum", [128, 512], F32),
-    "ps": ("psum", [128, 512], F32), "pd": ("psum", [128, 512], F32), "pa": ("psum", [128, 512], F32), "pb": ("psum", [128, 512], F32),
-}
-SEMAPHORES = ["sv", "ss", "st", "sg", "lx", "lu", "lw", "so", "sp", "loc", "earr", "arr0", "arr1"]
+SCRATCH = {n: _sb(512, BF) for n in ("xb", "wb", "ut", "ct", "rt", "bt", "kw", "kt")}
+SCRATCH.update({"ub": _sb(4, BF), "ew": _sb(520, BF), "mt": _sb(2048, BF), "dif": _sb(128, BF), "dm": _sb(128, BF)})
+for _n, _w in (("u", 128), ("w", 128), ("e", 512), ("mt", 512), ("c", 128), ("kw", 128), ("kt", 128)):
+    SCRATCH.update({_n + "q": _sb(_w, CODE), _n + "s": _sb(_w, PLANE)})
+for _n, _w in (("x%s0", 384), ("x%s1", 128), ("x%s2", 128), ("m%s0", 128), ("m%s1", 128)):
+    SCRATCH.update({_n % "q": _sb(_w, CODE), _n % "s": _sb(_w, PLANE)})
+SCRATCH.update({n: _sb(128, F32) for n in ("phi", "fac", "af", "y0", "y1")})
+SCRATCH.update({n: _sb(4, F32) for n in ("thr", "free", "pl0", "pl1")})
+SCRATCH.update({n: _sb(NH, BF) for n in ("up", "two", "zr", "hf", "hs")})
+SCRATCH.update({"nil": _sb(16, F32), "off0": _sb(2, "uint16"), "off1": _sb(2, "uint16")})
+SCRATCH.update({n: ("psum", [128, 512], F32) for n in ("pr0", "pr1", "pr2", "pr3", "ps", "pd", "pa", "pb")})
+SEMAPHORES = ["sv", "ss", "st", "sg", "lx", "lu", "lw", "so", "sp", "loc", "earr", "arr0", "arr1", "rel0", "rel1"]
 
 
 def rank_program(g, core, T, topo):
@@ -66,12 +58,12 @@ def rank_program(g, core, T, topo):
 
     peers = [d for d in T.cores if d != core]
     mate = [d for d in topo.cores_of(core) if d in peers][0]
-    far = sorted([d for d in peers if d != mate], key=lambda d: (-((T.rank_of(d) ^ rank) >> 1), T.rank_of(d) ^ rank))
+    far = sorted([d for d in peers if d != mate], key=lambda d: (topo.mates(core, d), topo.same_plane(core, d), topo.die(d) == topo.die(core)))
+    hand = far[5]
     fmask = topo.mask(core, mate)
     for d in far:
         fmask &= topo.mask(core, d)
-    near = [e for e in topo.engines(core, mate) if not fmask >> e & 1]
-    nmask = (1 << near[0]) | (1 << near[len(near) // 2])
+    nmask = topo.mask(core, mate) - fmask
     bits = lambda m: bin(m).count("1")
     half = 0 if core < mate else 1
 
@@ -79,20 +71,18 @@ def rank_program(g, core, T, topo):
         rid, pid = topo.addr(d, core)
         return DstId(rid=rid, pnc=pid)
 
-    def send(src, s, *groups):
+    def send(s, *groups):
         g.remote_dma_fused([RemoteDMATransfer(dst_ids=[dst(d) for d in to], dma_engine_mask=m, remote_sem=sem[s],
-                                              srcs=[src], dsts=[src for d in to]) for to, m in groups], local_sem=sem.loc)
-        count["loc"] = count.get("loc", 0) + sum(bits(m) for to, m in groups)
+                                              srcs=[src], dsts=[src for d in to]) for src, to, m in groups], local_sem=sem.loc)
+        count["loc"] = count.get("loc", 0) + sum(bits(m) for src, to, m in groups)
 
     def codes(b, a, e):
         return T[b][:, a:e].bitcast(dt.uint8)
 
-    enum, anum = bits(fmask) + bits(nmask), 2 * (6 * bits(fmask) + bits(nmask))
+    enum, anum, rnum = bits(fmask) + bits(nmask), 10 * bits(fmask) + 3 * bits(nmask), bits(fmask)
 
-    lu = done(g.scalar.dma_start(T.ub[:], T.u[:]), "lu", 16)
-    lx = done(g.sync.dma_start(T.xb[:], T.x[:]), "lx", 16)
-    need("y", lx)
-    lw = done(g.sync.dma_start(T.wb[:], T.w[:]), "lw", 16)
+    lu = done(g.sync.dma_start(T.ub[:], T.u[:]), "lu", 16)
+    lx = done(g.scalar.dma_start(T.xb[:], T.x[:]), "lx", 16)
 
     G = lambda ins: done(ins, "sg")
     small = {"allow_small_or_imprecise_dtypes": True}
@@ -100,73 +90,71 @@ def rank_program(g, core, T, topo):
     kk = G(g.iota(T.kw[:, 3:512:4], [[0, 8], [-2, 16]], 0, 0, **small))
 
     ve = V(g.vector.memset(T.ew[:], 0.0))
-    vb = V(g.vector.memset(T.bt[:], -0.25 * TINY))
+    V(g.vector.memset(T.bt[:], -0.25 * TINY))
     need("v", ve, kj)
     ve = V(g.vector.tensor_scalar(T.ew[:, 3:515:4], T.dif[:], 0.0, -4.0, A.is_equal, A.mult))
-    vs = V(g.vector.memset(T.sgn[:], 1.0))
+    V(g.vector.memset(T.kt[:, 3:512:4], 1.0))
     need("v", ve)
 
     def make_e(b):
         return V(g.vector.quantize_mx(T.eq[:, 128 * b:128 * b + 128], T.es[:, 128 * b:128 * b + 128], T.ew[:, 3 - b:515 - b]))
 
     te = make_e(half)
+    need("y", te)
+    lw = done(g.sync.dma_start(T.wb[:], T.w[:]), "lw", 16)
     need("g", te)
-    send(codes("eq", 128 * half, 128 * half + 128), "earr", ([mate], fmask))
-    send(T.es[:, 128 * half:128 * half + 128], "earr", ([mate], nmask))
+    send("earr", (T.es[:, 128 * half:128 * half + 128], [mate], fmask))
+    send("earr", (codes("eq", 128 * half, 128 * half + 128), [mate], nmask))
     eh = (T.eq[:, 128 * half:128 * half + 128], T.es[:, 128 * half:128 * half + 128])
 
     def zeros(out):
         return S(g.scalar.activation(out, T.ew[:, 0:512], F.Copy, scale=0.0))
 
-    need("s", ve)
-    zeros(T.ct[:])
-    for i in range(3):
-        zeros(T.mt[:, 512 * i:512 * i + 512])
+    need("s", kj)
+    for b, c in enumerate((256.0, 256.0, 1.0)):
+        sk = S(g.scalar.activation(T.kw[:, b:512:4], T.dif[:], F.Identity, bias=c, scale=0.0))
     qb = V(g.vector.quantize_mx(T.xq0[:, 128:256], T.xs0[:, 128:256], T.bt[:]))
-    need("v", vs)
-    vs = V(g.vector.memset(T.sgn[:, 1:2], -1.0))
-    need("v", lu, vs)
-    for i in range(4):
-        v = V(g.vector.tensor_scalar(T.ut[:, i:512:4], T.sgn[:], T.ub[:, i:i + 1], None, A.mult))
-    V(g.vector.memset(T.kw[:, 0:512:4], 256.0))
-    need("v", v)
-    tu = V(g.vector.quantize_mx(T.uq[:], T.us[:], T.ut[:]))
+    need("v", kk, lu)
+    need("s", ve, lu)
+    for i in range(3):
+        v = V(g.vector.tensor_scalar(T.ut[:, i:512:4], T.dif[:], 0.0, T.ub[:, i:i + 1], A.mult, A.add))
+    s = S(g.scalar.activation(T.ut[:, 3:512:4], T.dif[:], F.Identity, bias=T.ub[:, 3:4], scale=0.0))
+    zeros(T.ct[:])
     need("v", lx)
     tx = V(g.vector.quantize_mx(T.xq0[:, 256:384], T.xs0[:, 256:384], T.xb[:]))
+    need("v", v, s)
+    tu = V(g.vector.quantize_mx(T.uq[:], T.us[:], T.ut[:]))
     vf = V(g.vector.tensor_scalar(T.fac[:], T.dif[:], 0.0, 1.0 - 2.0 ** -24, A.is_le, A.max))
-    V(g.vector.memset(T.kw[:, 1:512:4], 256.0))
-    V(g.vector.memset(T.kw[:, 2:512:4], 1.0))
-    V(g.vector.memset(T.kt[:, 3:512:4], 1.0))
-    vk = V(g.vector.tensor_scalar(T.kt[:, 2:512:4], T.dif[:], 0.0, None, A.is_gt))
+    V(g.vector.quantize_mx(T.kwq[:], T.kws[:], T.kw[:]))
 
     def floor(bank):
         M(bank[:, 0:130], eh[0], eh[1], T.xq0[:, 128:258], T.xs0[:, 128:258], True, False)
 
     own = (K * rank, K * rank + K)
-    sread, ty, sy = [], None, None
+    sy = None
     for t in range(R):
         x0 = 0 if t else 256
         xq, xs = T["xq%d" % t][:, x0:x0 + 128], T["xs%d" % t][:, x0:x0 + 128]
         mq, ms = "mq%d" % t, "ms%d" % t
         off, pl = T["off%d" % t], T["pl%d" % t]
-        need("t", tu, tx, *sread)
+        need("t", tx)
         if t == 0:
             floor(T.ps)
+        need("t", tu)
         ts = M(T.ps[:, 0:128], T.uq[:], T.us[:], xq, xs, False, True)
         tc = M(T.pa[:, 0:128], xq, xs, T.uq[:], T.us[:], t == 0, True)
-        need("v", ts, vf)
-        V(g.vector.tensor_tensor(T.af[:], T.ps[:, 0:128], T.fac[:], A.mult))
-        need("v", tc)
+        need("v", vf, ts)
+        v = V(g.vector.tensor_tensor(T.af[:], T.ps[:, 0:128], T.fac[:], A.mult))
+        need("s", tc)
         if t == 0:
-            v = V(g.vector.tensor_scalar(T.thr[:, 0:1], T.pa[:, 0:1], T.pa[:, 1:2], TINY, A.max, A.max))
+            V(g.vector.tensor_scalar(T.kt[:, 2:512:4], T.dif[:], 0.0, None, A.is_gt))
+            s = S(g.scalar.activation(T.thr[:, 0:1], T.pa[:, 0:1], F.Abs, bias=TINY))
+            zeros(T.mt[:, 0:512])
         else:
-            v = V(g.vector.tensor_scalar(T.thr[:, 0:1], T.pa[:, 0:1], T.pa[:, 1:2], T.free[:, 0:1], A.max, A.mult))
-        need("v", v)
+            s = S(g.scalar.activation(T.thr[:, 0:1], T.pa[:, 0:1], F.Abs, scale=T.free[:, 0:1]))
+        need("v", v, s)
         V(g.vector.tensor_scalar(T.kt[:, 0:512:4], T.af[:], T.thr[:, 0:1], 1.0, A.is_lt, A.subtract))
         v = V(g.vector.tensor_scalar(T.kt[:, 1:512:4], T.af[:], -1.0, T.thr[:, 0:1], A.mult, A.is_lt))
-        if t == 0:
-            need("v", kk)
-            V(g.vector.quantize_mx(T.kwq[:], T.kws[:], T.kw[:]))
         need("v", v)
         qk = V(g.vector.quantize_mx(T.ktq[:], T.kts[:], T.kt[:]))
         need("t", qk)
@@ -174,27 +162,28 @@ def rank_program(g, core, T, topo):
         if t == 0:
             tr = M(T.pa[:, 0:128], T.ktq[:], T.kts[:], T.kwq[:], T.kws[:])
             V(g.vector.memset(T.two[:], 2.0))
-            vz = V(g.vector.memset(T.zr[:], 0.0))
-            V(g.vector.memset(T.phi[:], 1.0))
+            V(g.vector.memset(T.zr[:], 0.0))
         need("v", tk)
         voff = V(g.vector.tensor_reduce(off[:, 0:1], T.pb[:, 0:128], AxisListType.X, A.min, apply_absolute_value=True))
         need("v", voff)
+        tq = V(g.vector.tensor_copy(T[ms][:, own[0]:own[1]], xs.indirect(off[:, 0:1])))
         tp = V(g.vector.tensor_copy(T[mq][:, own[0]:own[1]].bitcast(dt.uint32), xq.bitcast(dt.uint32).indirect(off[:, 0:1])))
-        need("s", voff)
-        tq = S(g.scalar.activation(T[ms][:, own[0]:own[1]], xs.indirect(off[:, 0:1]), F.Copy))
-        need("g", tp)
-        send(codes(mq, own[0], own[1]), "arr%d" % t, (far, fmask), ([mate], nmask))
+        arr, rel = "arr%d" % t, "rel%d" % t
+        cq, cs = codes(mq, own[0], own[1]), T[ms][:, own[0]:own[1]]
         need("g", tq)
-        send(T[ms][:, own[0]:own[1]], "arr%d" % t, (far, fmask), ([mate], nmask))
-        def copy_y(r):
-            need("s", ty)
-            s = S(g.scalar.activation(T["y%d" % r][:], T.pd[:, 0:128], F.Copy))
-            need("y", s)
-            done(g.sync.dma_start(T.y[:, P * r:P * r + P], T["y%d" % r][:]), "so", 16)
-            return s
-
+        send(rel, (cs, [hand], fmask))
+        send(arr, (cs, far[:2], fmask), (cs, [mate], nmask))
+        need("g", tp)
+        send(arr, (cq, far[:4], fmask), (cq, [mate], nmask))
+        send(arr, (cs, far[2:4], fmask))
+        send(arr, (cq, far[4:], fmask))
+        need("g", (rel, rnum))
+        send(arr, (T[ms][:, K * T.rank_of(hand):K * T.rank_of(hand) + K], [mate], nmask))
         if t == 0:
-            zm = zeros(T.mt[:, 1536:2048])
+            zeros(T.mt[:, 512:1024])
+            zm = zeros(T.mt[:, 1024:1536])
+            V(g.vector.memset(T.phi[:], 1.0))
+            V(g.vector.memset(T.mt[:, 1536:2048], 0.0))
             v = V(g.vector.tensor_scalar(T.bt[:, half:512:4], T.dif[:], 0.0, BIG, A.not_equal, A.mult))
             make_e(2)
             te = make_e(3)
@@ -203,11 +192,7 @@ def rank_program(g, core, T, topo):
             V(g.vector.memset(T.phi[:, 127:128], 1.0 + 3.0 / 256))
             V(g.vector.tensor_tensor_scan(T.up[:], T.two[:], T.zr[:], 2.0 ** -64 * (1.0 + 1.0 / 64), A.mult, A.max))
             vn = V(g.vector.memset(T.nil[:], 0.0))
-        else:
-            sy = copy_y(0)
-        vp = V(g.vector.tensor_copy(pl[0:32, 0:1], off[0:32, 0:1]))
-        need("y", vp)
-        done(g.sync.dma_start(T.pl[0:1, K * t:K * t + K], pl[0:16, 0:1]), "so", 16)
+        vp = vl = V(g.vector.tensor_copy(pl[0:32, 0:1], off[0:32, 0:1]))
         if t == 0:
             need("v", tr, lw, vn)
             vp = V(g.vector.tensor_scalar(T.free[:, 0:1], T.pa[:, 0:1], 4096.0, None, A.is_ge))
@@ -219,12 +204,12 @@ def rank_program(g, core, T, topo):
         if sy:
             need("t", sy)
         M(T.pd[:, 0:258], eh[0], eh[1], T.xq0[:, 0:258], T.xs0[:, 0:258], True, False)
-        need("t", tp, vp, tq, ("arr%d" % t, anum))
+        need("t", tp, vp, tw, tq, (rel, rnum), (arr, anum))
         td = M(T.pd[:, 0:128], T[mq][:], T[ms][:], T[mq][:], T[ms][:], False, True)
         ta = M(T.pa[:, 0:128], T[mq][:], T[ms][:], T.eq[:, 0:128], T.es[:, 0:128])
         tb = M(T.pb[:, 0:384], T[mq][:], T[ms][:], T.eq[:, 128:512], T.es[:, 128:512])
         tg = M(T.ps[:, 0:128], T[mq][:], T[ms][:], xq, xs)
-        need("s", zm, ta, ("sv", count["sv"]))
+        need("s", zm, ("sv", count["sv"]), ta)
         sa = S(g.scalar.activation(T.mt[:, 0:512:4], T.pa[:, 0:128], F.Copy, scale=-0.25))
         need("s", tb)
         s1 = S(g.scalar.activation(T.mt[:, 512:1024:4], T.pb[:, 0:128], F.Copy, scale=-0.25))
@@ -234,31 +219,36 @@ def rank_program(g, core, T, topo):
             need("v", (sa, s1, sb, sb)[b])
             return V(g.vector.quantize_mx(T.mtq[:, 128 * b:128 * b + 128], T.mts[:, 128 * b:128 * b + 128], T.mt[:, 512 * b:512 * b + 512]))
 
-        need("v", td, zm, ("sv", count["sv"]))
+        need("v", zm, ("sv", count["sv"]), td)
         vd = V(g.vector.tensor_tensor_scan(T.dm[:], T.pd[:, 0:128], T.phi[:], 0.0, A.max, A.mult))
         need("v", vd)
         v = V(g.vector.tensor_scalar(T.hf[:], T.up[:], T.dm[:, 127:128], 0.5, A.is_gt, A.max))
         need("v", v)
         v = V(g.vector.tensor_tensor_scan(T.hs[:], T.hf[:], T.zr[:], 2.0 ** 64, A.mult, A.max))
         qm = [turned(0)]
-        need("v", v, tg)
+        need("v", tg, v)
         vc = V(g.vector.tensor_scalar(T.ct[:, 0:512:4], T.ps[:, 0:128], T.hs[:, NH - 1:NH], None, A.mult))
         qm.append(turned(1))
         need("v", vc)
         qc = V(g.vector.quantize_mx(T.cq[:], T.cs[:], T.ct[:]))
         qm += [turned(2), turned(3)]
-        need("t", tw, vd)
+        need("t", vd)
         ty = M(T.pd[:, 0:128], T.wq[:], T.ws[:], T[mq][:], T[ms][:])
-        if t:
-            copy_y(t)
-        else:
-            need("t", vc, sa)
-            floor(T.ps)
+        need("s", ty)
+        sy = S(g.scalar.activation(T["y%d" % t][:], T.pd[:, 0:128], F.Copy))
+        need("y", vl, sy)
+        done(g.sync.dma_start(T.y[:, P * t:P * t + P], T["y%d" % t][:]), "so", 16)
+        done(g.sync.dma_start(T.pl[0:1, K * t:K * t + K], pl[0:16, 0:1]), "so", 16)
+        if t == 0:
+            need("t", sa)
             floor(T.pa)
+            need("t", vc)
+            floor(T.ps)
         tz = []
         for b in range(4):
             need("t", qc, qm[b])
             tz.append(M(T["pr%d" % b][:, 0:128], T.mtq[:, 128 * b:128 * b + 128], T.mts[:, 128 * b:128 * b + 128], T.cq[:], T.cs[:], False, True))
+        need("t", sb)
         for b in range(4):
             q = "ssvv"[b]
             need(q, tz[b])
@@ -269,7 +259,6 @@ def rank_program(g, core, T, topo):
                 v = V(g.vector.tensor_scalar(out, src, -0.25, None, A.mult))
         need("v", s, v)
         tx = V(g.vector.quantize_mx(T["xq%d" % (t + 1)][:], T["xs%d" % (t + 1)][:], T.rt[:]))
-        sread = [sa, sb]
 
     need("y", tx)
     need("s", tx)
@@ -278,5 +267,6 @@ def rank_program(g, core, T, topo):
     for k in range(4):
         q, s = (g.scalar, "sp") if k % 2 == 0 else (g.sync, "so")
         done(q.dma_start(T.osc[4 * k:4 * k + 4, :], xs[32 * k:32 * k + 4, :]), s, 16)
-    need("g", *[(s, n) for s, n in count.items()])
-    need("g", ("earr", enum), ("arr0", anum), ("arr1", anum))
+    need("g", ("earr", enum), ("arr0", anum), ("arr1", anum), *[(s, n) for s, n in count.items() if s not in ("so", "sp")])
+    need("y", ("so", count["so"]))
+    need("s", ("sp", count["sp"]))

import numpy as np
from concourse.bass import DstId, RemoteDMATransfer
from concourse.mybir import dt, AluOpType, AxisListType, ActivationFunctionType

P, K, R = 128, 16, 2
CODE, PLANE, BF, F32 = "float8_e4m3fn_x4", "uint8", "bfloat16", "float32"
TINY = 2.0 ** -120
BIG = 2.0 ** 80
NH = 136


def _sb(n, d):
    return ("sbuf", [128, n], d)


SCRATCH = {n: _sb(512, BF) for n in ("xb", "wb", "ut", "ct", "rt", "bt", "kw", "kt")}
SCRATCH.update({"ub": _sb(4, BF), "ew": _sb(520, BF), "mt": _sb(2048, BF), "dif": _sb(128, BF), "dm": _sb(128, BF)})
for _n, _w in (("u", 128), ("w", 128), ("e", 512), ("mt", 512), ("c", 128), ("kw", 128), ("kt", 128)):
    SCRATCH.update({_n + "q": _sb(_w, CODE), _n + "s": _sb(_w, PLANE)})
for _n, _w in (("x%s0", 384), ("x%s1", 128), ("x%s2", 128), ("m%s0", 128), ("m%s1", 128)):
    SCRATCH.update({_n % "q": _sb(_w, CODE), _n % "s": _sb(_w, PLANE)})
SCRATCH.update({n: _sb(128, F32) for n in ("phi", "fac", "af", "y0", "y1")})
SCRATCH.update({n: _sb(4, F32) for n in ("thr", "free", "pl0", "pl1")})
SCRATCH.update({n: _sb(NH, BF) for n in ("up", "two", "zr", "hf", "hs")})
SCRATCH.update({"nil": _sb(16, F32), "off0": _sb(2, "uint16"), "off1": _sb(2, "uint16")})
SCRATCH.update({n: ("psum", [128, 512], F32) for n in ("pr0", "pr1", "pr2", "pr3", "ps", "pd", "pa", "pb")})
SEMAPHORES = ["sv", "ss", "st", "sg", "lx", "lu", "lw", "so", "sp", "loc", "earr", "arr0", "arr1", "rel0", "rel1"]


def rank_program(g, core, T, topo):
    rank = T.rank_of(core)
    if rank is None:
        return
    A, F = AluOpType, ActivationFunctionType
    sem = T.sem
    queues = {"v": g.vector, "s": g.scalar, "t": g.tensor, "g": g, "y": g.sync}
    count, seen = {}, {}

    def need(q, *toks):
        for s, n in toks:
            if seen.get((q, s), 0) < n:
                queues[q].wait_ge(sem[s], n)
                seen[(q, s)] = n

    def done(ins, s, n=1):
        count[s] = count.get(s, 0) + n
        ins.then_inc(sem[s], n)
        return (s, count[s])

    def V(ins):
        return done(ins, "sv")

    def S(ins):
        return done(ins, "ss")

    def M(out, l, ls, r, rs, start=True, stop=True):
        return done(g.tensor.matmul_mx(out, l, ls, r, rs, start, stop), "st")

    peers = [d for d in T.cores if d != core]
    mate = [d for d in topo.cores_of(core) if d in peers][0]
    far = sorted([d for d in peers if d != mate], key=lambda d: (topo.mates(core, d), topo.same_plane(core, d), topo.die(d) == topo.die(core)))
    hand = far[5]
    fmask = topo.mask(core, mate)
    for d in far:
        fmask &= topo.mask(core, d)
    nmask = topo.mask(core, mate) - fmask
    bits = lambda m: bin(m).count("1")
    half = 0 if core < mate else 1

    def dst(d):
        rid, pid = topo.addr(d, core)
        return DstId(rid=rid, pnc=pid)

    def send(s, *groups):
        g.remote_dma_fused([RemoteDMATransfer(dst_ids=[dst(d) for d in to], dma_engine_mask=m, remote_sem=sem[s],
                                              srcs=[src], dsts=[src for d in to]) for src, to, m in groups], local_sem=sem.loc)
        count["loc"] = count.get("loc", 0) + sum(bits(m) for src, to, m in groups)

    def codes(b, a, e):
        return T[b][:, a:e].bitcast(dt.uint8)

    enum, anum, rnum = bits(fmask) + bits(nmask), 10 * bits(fmask) + 3 * bits(nmask), bits(fmask)

    lu = done(g.sync.dma_start(T.ub[:], T.u[:]), "lu", 16)
    lx = done(g.scalar.dma_start(T.xb[:], T.x[:]), "lx", 16)

    G = lambda ins: done(ins, "sg")
    small = {"allow_small_or_imprecise_dtypes": True}
    kj = G(g.iota(T.dif[:], [[1, 128]], 0, -1, **small))
    kk = G(g.iota(T.kw[:, 3:512:4], [[0, 8], [-2, 16]], 0, 0, **small))

    ve = V(g.vector.memset(T.ew[:], 0.0))
    V(g.vector.memset(T.bt[:], -0.25 * TINY))
    need("v", ve, kj)
    ve = V(g.vector.tensor_scalar(T.ew[:, 3:515:4], T.dif[:], 0.0, -4.0, A.is_equal, A.mult))
    V(g.vector.memset(T.kt[:, 3:512:4], 1.0))
    need("v", ve)

    def make_e(b):
        return V(g.vector.quantize_mx(T.eq[:, 128 * b:128 * b + 128], T.es[:, 128 * b:128 * b + 128], T.ew[:, 3 - b:515 - b]))

    te = make_e(half)
    need("y", te)
    lw = done(g.sync.dma_start(T.wb[:], T.w[:]), "lw", 16)
    need("g", te)
    send("earr", (T.es[:, 128 * half:128 * half + 128], [mate], fmask))
    send("earr", (codes("eq", 128 * half, 128 * half + 128), [mate], nmask))
    eh = (T.eq[:, 128 * half:128 * half + 128], T.es[:, 128 * half:128 * half + 128])

    def zeros(out):
        return S(g.scalar.activation(out, T.ew[:, 0:512], F.Copy, scale=0.0))

    need("s", kj)
    for b, c in enumerate((256.0, 256.0, 1.0)):
        sk = S(g.scalar.activation(T.kw[:, b:512:4], T.dif[:], F.Identity, bias=c, scale=0.0))
    qb = V(g.vector.quantize_mx(T.xq0[:, 128:256], T.xs0[:, 128:256], T.bt[:]))
    need("v", kk, lu)
    need("s", ve, lu)
    for i in range(3):
        v = V(g.vector.tensor_scalar(T.ut[:, i:512:4], T.dif[:], 0.0, T.ub[:, i:i + 1], A.mult, A.add))
    s = S(g.scalar.activation(T.ut[:, 3:512:4], T.dif[:], F.Identity, bias=T.ub[:, 3:4], scale=0.0))
    zeros(T.ct[:])
    need("v", lx)
    tx = V(g.vector.quantize_mx(T.xq0[:, 256:384], T.xs0[:, 256:384], T.xb[:]))
    need("v", v, s)
    tu = V(g.vector.quantize_mx(T.uq[:], T.us[:], T.ut[:]))
    vf = V(g.vector.tensor_scalar(T.fac[:], T.dif[:], 0.0, 1.0 - 2.0 ** -24, A.is_le, A.max))
    V(g.vector.quantize_mx(T.kwq[:], T.kws[:], T.kw[:]))

    def floor(bank):
        M(bank[:, 0:130], eh[0], eh[1], T.xq0[:, 128:258], T.xs0[:, 128:258], True, False)

    own = (K * rank, K * rank + K)
    sy = None
    for t in range(R):
        x0 = 0 if t else 256
        xq, xs = T["xq%d" % t][:, x0:x0 + 128], T["xs%d" % t][:, x0:x0 + 128]
        mq, ms = "mq%d" % t, "ms%d" % t
        off, pl = T["off%d" % t], T["pl%d" % t]
        need("t", tx)
        if t == 0:
            floor(T.ps)
        need("t", tu)
        ts = M(T.ps[:, 0:128], T.uq[:], T.us[:], xq, xs, False, True)
        tc = M(T.pa[:, 0:128], xq, xs, T.uq[:], T.us[:], t == 0, True)
        need("v", vf, ts)
        v = V(g.vector.tensor_tensor(T.af[:], T.ps[:, 0:128], T.fac[:], A.mult))
        need("s", tc)
        if t == 0:
            V(g.vector.tensor_scalar(T.kt[:, 2:512:4], T.dif[:], 0.0, None, A.is_gt))
            s = S(g.scalar.activation(T.thr[:, 0:1], T.pa[:, 0:1], F.Abs, bias=TINY))
            zeros(T.mt[:, 0:512])
        else:
            s = S(g.scalar.activation(T.thr[:, 0:1], T.pa[:, 0:1], F.Abs, scale=T.free[:, 0:1]))
        need("v", v, s)
        V(g.vector.tensor_scalar(T.kt[:, 0:512:4], T.af[:], T.thr[:, 0:1], 1.0, A.is_lt, A.subtract))
        v = V(g.vector.tensor_scalar(T.kt[:, 1:512:4], T.af[:], -1.0, T.thr[:, 0:1], A.mult, A.is_lt))
        need("v", v)
        qk = V(g.vector.quantize_mx(T.ktq[:], T.kts[:], T.kt[:]))
        need("t", qk)
        tk = M(T.pb[:, 0:128], T.kwq[:], T.kws[:], T.ktq[:], T.kts[:])
        if t == 0:
            tr = M(T.pa[:, 0:128], T.ktq[:], T.kts[:], T.kwq[:], T.kws[:])
            V(g.vector.memset(T.two[:], 2.0))
            V(g.vector.memset(T.zr[:], 0.0))
        need("v", tk)
        voff = V(g.vector.tensor_reduce(off[:, 0:1], T.pb[:, 0:128], AxisListType.X, A.min, apply_absolute_value=True))
        need("v", voff)
        tq = V(g.vector.tensor_copy(T[ms][:, own[0]:own[1]], xs.indirect(off[:, 0:1])))
        tp = V(g.vector.tensor_copy(T[mq][:, own[0]:own[1]].bitcast(dt.uint32), xq.bitcast(dt.uint32).indirect(off[:, 0:1])))
        arr, rel = "arr%d" % t, "rel%d" % t
        cq, cs = codes(mq, own[0], own[1]), T[ms][:, own[0]:own[1]]
        need("g", tq)
        send(rel, (cs, [hand], fmask))
        send(arr, (cs, far[:2], fmask), (cs, [mate], nmask))
        need("g", tp)
        send(arr, (cq, far[:4], fmask), (cq, [mate], nmask))
        send(arr, (cs, far[2:4], fmask))
        send(arr, (cq, far[4:], fmask))
        need("g", (rel, rnum))
        send(arr, (T[ms][:, K * T.rank_of(hand):K * T.rank_of(hand) + K], [mate], nmask))
        if t == 0:
            zeros(T.mt[:, 512:1024])
            zm = zeros(T.mt[:, 1024:1536])
            V(g.vector.memset(T.phi[:], 1.0))
            V(g.vector.memset(T.mt[:, 1536:2048], 0.0))
            v = V(g.vector.tensor_scalar(T.bt[:, half:512:4], T.dif[:], 0.0, BIG, A.not_equal, A.mult))
            make_e(2)
            te = make_e(3)
            need("v", v)
            qb = V(g.vector.quantize_mx(T.xq0[:, 0:128], T.xs0[:, 0:128], T.bt[:]))
            V(g.vector.memset(T.phi[:, 127:128], 1.0 + 3.0 / 256))
            V(g.vector.tensor_tensor_scan(T.up[:], T.two[:], T.zr[:], 2.0 ** -64 * (1.0 + 1.0 / 64), A.mult, A.max))
            vn = V(g.vector.memset(T.nil[:], 0.0))
        vp = vl = V(g.vector.tensor_copy(pl[0:32, 0:1], off[0:32, 0:1]))
        if t == 0:
            need("v", tr, lw, vn)
            vp = V(g.vector.tensor_scalar(T.free[:, 0:1], T.pa[:, 0:1], 4096.0, None, A.is_ge))
            tw = V(g.vector.quantize_mx(T.wq[:], T.ws[:], T.wb[:]))
            V(g.vector.tensor_copy(T.fac[:, 0:128].indirect(off[:, 0:1]), T.nil[:]))
        need("t", te, qb, ("earr", enum))
        for b in range(4):
            M(T["pr%d" % b][:, 0:128], T.eq[:, 128 * b:128 * b + 128], T.es[:, 128 * b:128 * b + 128], xq, xs, True, False)
        if sy:
            need("t", sy)
        M(T.pd[:, 0:258], eh[0], eh[1], T.xq0[:, 0:258], T.xs0[:, 0:258], True, False)
        need("t", tp, vp, tw, tq, (rel, rnum), (arr, anum))
        td = M(T.pd[:, 0:128], T[mq][:], T[ms][:], T[mq][:], T[ms][:], False, True)
        ta = M(T.pa[:, 0:128], T[mq][:], T[ms][:], T.eq[:, 0:128], T.es[:, 0:128])
        tb = M(T.pb[:, 0:384], T[mq][:], T[ms][:], T.eq[:, 128:512], T.es[:, 128:512])
        tg = M(T.ps[:, 0:128], T[mq][:], T[ms][:], xq, xs)
        need("s", zm, ("sv", count["sv"]), ta)
        sa = S(g.scalar.activation(T.mt[:, 0:512:4], T.pa[:, 0:128], F.Copy, scale=-0.25))
        need("s", tb)
        s1 = S(g.scalar.activation(T.mt[:, 512:1024:4], T.pb[:, 0:128], F.Copy, scale=-0.25))
        sb = S(g.scalar.activation(T.mt[:, 1024:2048:4], T.pb[:, 128:384], F.Copy, scale=-0.25))

        def turned(b):
            need("v", (sa, s1, sb, sb)[b])
            return V(g.vector.quantize_mx(T.mtq[:, 128 * b:128 * b + 128], T.mts[:, 128 * b:128 * b + 128], T.mt[:, 512 * b:512 * b + 512]))

        need("v", zm, ("sv", count["sv"]), td)
        vd = V(g.vector.tensor_tensor_scan(T.dm[:], T.pd[:, 0:128], T.phi[:], 0.0, A.max, A.mult))
        need("v", vd)
        v = V(g.vector.tensor_scalar(T.hf[:], T.up[:], T.dm[:, 127:128], 0.5, A.is_gt, A.max))
        need("v", v)
        v = V(g.vector.tensor_tensor_scan(T.hs[:], T.hf[:], T.zr[:], 2.0 ** 64, A.mult, A.max))
        qm = [turned(0)]
        need("v", tg, v)
        vc = V(g.vector.tensor_scalar(T.ct[:, 0:512:4], T.ps[:, 0:128], T.hs[:, NH - 1:NH], None, A.mult))
        qm.append(turned(1))
        need("v", vc)
        qc = V(g.vector.quantize_mx(T.cq[:], T.cs[:], T.ct[:]))
        qm += [turned(2), turned(3)]
        need("t", vd)
        ty = M(T.pd[:, 0:128], T.wq[:], T.ws[:], T[mq][:], T[ms][:])
        need("s", ty)
        sy = S(g.scalar.activation(T["y%d" % t][:], T.pd[:, 0:128], F.Copy))
        need("y", vl, sy)
        done(g.sync.dma_start(T.y[:, P * t:P * t + P], T["y%d" % t][:]), "so", 16)
        done(g.sync.dma_start(T.pl[0:1, K * t:K * t + K], pl[0:16, 0:1]), "so", 16)
        if t == 0:
            need("t", sa)
            floor(T.pa)
            need("t", vc)
            floor(T.ps)
        tz = []
        for b in range(4):
            need("t", qc, qm[b])
            tz.append(M(T["pr%d" % b][:, 0:128], T.mtq[:, 128 * b:128 * b + 128], T.mts[:, 128 * b:128 * b + 128], T.cq[:], T.cs[:], False, True))
        need("t", sb)
        for b in range(4):
            q = "ssvv"[b]
            need(q, tz[b])
            src, out = T["pr%d" % b][:, 0:128], T.rt[:, b:512:4]
            if q == "s":
                s = S(g.scalar.activation(out, src, F.Copy, scale=-0.25))
            else:
                v = V(g.vector.tensor_scalar(out, src, -0.25, None, A.mult))
        need("v", s, v)
        tx = V(g.vector.quantize_mx(T["xq%d" % (t + 1)][:], T["xs%d" % (t + 1)][:], T.rt[:]))

    need("y", tx)
    need("s", tx)
    xs = T["xs%d" % R]
    done(g.sync.dma_start(T.oc[:], codes("xq%d" % R, 0, 128)), "so", 16)
    for k in range(4):
        q, s = (g.scalar, "sp") if k % 2 == 0 else (g.sync, "so")
        done(q.dma_start(T.osc[4 * k:4 * k + 4, :], xs[32 * k:32 * k + 4, :]), s, 16)
    need("g", ("earr", enum), ("arr0", anum), ("arr1", anum), *[(s, n) for s, n in count.items() if s not in ("so", "sp")])
    need("y", ("so", count["so"]))
    need("s", ("sp", count["sp"]))
